import numpy as np, ml_dtypes
CORES = [0,8,16,24,32,40,48,56,64,72,80,88,96,104,112,120]
N = 16
PERM = [[0,1],[1,0],[2,3],[3,2],[4,5],[5,4],[6,7],[7,6],[8,9],[9,8],[10,11],[11,10],[12,13],[13,12],[14,15],[15,14]]
def setup_inputs(rng):
    return {"x": rng.standard_normal((N, 128, 4), dtype=np.float32).astype(ml_dtypes.bfloat16)}
def reference(x):
    y = np.empty_like(x)
    for s, d in PERM:
        y[d] = x[s]
    return {"y": y}

@@ -1,0 +1,54 @@
+SCRATCH = {
+    "out": ("dram", [128, 4], "bfloat16"),
+    "relay": ("dram", [128, 4], "bfloat16"),
+    "land": ("dram", [128, 4], "bfloat16"),
+}
+SEMAPHORES = ["loaded", "stored", "arrived", "got", "passed"]
+
+ENGINE = 0x1
+
+
+def helper_of(src, dst, topo):
+    if topo.may_write(src, dst):
+        return src
+    base = topo.chip(src) * 8
+    able = [c for c in range(base, base + 8) if c != src and topo.may_write(c, dst)]
+    same_die = [c for c in able if topo.die(c) == topo.die(src)]
+    return (same_die or able)[0]
+
+
+def rank_program(g, core, T, topo):
+    cores = T.cores
+    routes = []
+    for s, d in T.tables["PERM"]:
+        routes.append((cores[s], helper_of(cores[s], cores[d], topo), cores[d]))
+
+    send = [r for r in routes if r[0] == core]
+    carry = [r for r in routes if r[1] == core and r[0] != core]
+    take = [r for r in routes if r[2] == core]
+
+    for route in carry:
+        rid, pid = topo.addr(route[2])[:2]
+        g.wait_ge(T.sem.got, 1)
+        g.remote_dma(T.land[:], T.relay[:], T.sem.arrived, T.sem.passed, pid, rid, ENGINE)
+        g.wait_ge(T.sem.passed, 1)
+
+    for route in send:
+        helper, dst = route[1], route[2]
+        if dst == core:
+            g.dma_start(T.y[:], T.x[:]).then_inc(T.sem.stored, 16)
+            g.wait_ge(T.sem.stored, 16)
+            return
+        g.dma_start(T.out[:], T.x[:]).then_inc(T.sem.loaded, 16)
+        g.wait_ge(T.sem.loaded, 16)
+        if helper == core:
+            rid, pid = topo.addr(dst)[:2]
+            g.remote_dma(T.land[:], T.out[:], T.sem.arrived, T.sem.arrived, pid, rid, ENGINE)
+        else:
+            rid, pid = topo.addr(helper)[:2]
+            g.remote_dma(T.relay[:], T.out[:], T.sem.got, T.sem.arrived, pid, rid, ENGINE)
+    if send or take:
+        g.wait_ge(T.sem.arrived, len(send) + len(take))
+    if take:
+        g.dma_start(T.y[:], T.land[:]).then_inc(T.sem.stored, 16)
+        g.wait_ge(T.sem.stored, 16)

@@ -5,7 +5,8 @@ SCRATCH = {
 }
 SEMAPHORES = ["loaded", "stored", "arrived", "got", "passed"]
 
-ENGINE = 0x1
+ON_CHIP = 1
+OFF_CHIP = 1
 
 
 def helper_of(src, dst, topo):
@@ -27,12 +28,17 @@ def rank_program(g, core, T, topo):
     carry = [r for r in routes if r[1] == core and r[0] != core]
     take = [r for r in routes if r[2] == core]
 
+    def engines(a, b):
+        return ON_CHIP if topo.chip(a) == topo.chip(b) else OFF_CHIP
+
     for route in carry:
         rid, pid = topo.addr(route[2])[:2]
-        g.wait_ge(T.sem.got, 1)
-        g.remote_dma(T.land[:], T.relay[:], T.sem.arrived, T.sem.passed, pid, rid, ENGINE)
-        g.wait_ge(T.sem.passed, 1)
+        n = engines(core, route[2])
+        g.wait_ge(T.sem.got, engines(route[0], core))
+        g.remote_dma(T.land[:], T.relay[:], T.sem.arrived, T.sem.passed, pid, rid, (1 << n) - 1)
+        g.wait_ge(T.sem.passed, n)
 
+    expected = 0
     for route in send:
         helper, dst = route[1], route[2]
         if dst == core:
@@ -43,12 +49,17 @@ def rank_program(g, core, T, topo):
         g.wait_ge(T.sem.loaded, 16)
         if helper == core:
             rid, pid = topo.addr(dst)[:2]
-            g.remote_dma(T.land[:], T.out[:], T.sem.arrived, T.sem.arrived, pid, rid, ENGINE)
+            n = engines(core, dst)
+            g.remote_dma(T.land[:], T.out[:], T.sem.arrived, T.sem.arrived, pid, rid, (1 << n) - 1)
         else:
             rid, pid = topo.addr(helper)[:2]
-            g.remote_dma(T.relay[:], T.out[:], T.sem.got, T.sem.arrived, pid, rid, ENGINE)
-    if send or take:
-        g.wait_ge(T.sem.arrived, len(send) + len(take))
+            n = engines(core, helper)
+            g.remote_dma(T.relay[:], T.out[:], T.sem.got, T.sem.arrived, pid, rid, (1 << n) - 1)
+        expected += n
+    for route in take:
+        expected += engines(route[1], core)
+    if expected:
+        g.wait_ge(T.sem.arrived, expected)
     if take:
         g.dma_start(T.y[:], T.land[:]).then_inc(T.sem.stored, 16)
         g.wait_ge(T.sem.stored, 16)

SCRATCH = {
    "out": ("dram", [128, 4], "bfloat16"),
    "relay": ("dram", [128, 4], "bfloat16"),
    "land": ("dram", [128, 4], "bfloat16"),
}
SEMAPHORES = ["loaded", "stored", "arrived", "got", "passed"]

ON_CHIP = 1
OFF_CHIP = 1


def helper_of(src, dst, topo):
    if topo.may_write(src, dst):
        return src
    base = topo.chip(src) * 8
    able = [c for c in range(base, base + 8) if c != src and topo.may_write(c, dst)]
    same_die = [c for c in able if topo.die(c) == topo.die(src)]
    return (same_die or able)[0]


def rank_program(g, core, T, topo):
    cores = T.cores
    routes = []
    for s, d in T.tables["PERM"]:
        routes.append((cores[s], helper_of(cores[s], cores[d], topo), cores[d]))

    send = [r for r in routes if r[0] == core]
    carry = [r for r in routes if r[1] == core and r[0] != core]
    take = [r for r in routes if r[2] == core]

    def engines(a, b):
        return ON_CHIP if topo.chip(a) == topo.chip(b) else OFF_CHIP

    for route in carry:
        rid, pid = topo.addr(route[2])[:2]
        n = engines(core, route[2])
        g.wait_ge(T.sem.got, engines(route[0], core))
        g.remote_dma(T.land[:], T.relay[:], T.sem.arrived, T.sem.passed, pid, rid, (1 << n) - 1)
        g.wait_ge(T.sem.passed, n)

    expected = 0
    for route in send:
        helper, dst = route[1], route[2]
        if dst == core:
            g.dma_start(T.y[:], T.x[:]).then_inc(T.sem.stored, 16)
            g.wait_ge(T.sem.stored, 16)
            return
        g.dma_start(T.out[:], T.x[:]).then_inc(T.sem.loaded, 16)
        g.wait_ge(T.sem.loaded, 16)
        if helper == core:
            rid, pid = topo.addr(dst)[:2]
            n = engines(core, dst)
            g.remote_dma(T.land[:], T.out[:], T.sem.arrived, T.sem.arrived, pid, rid, (1 << n) - 1)
        else:
            rid, pid = topo.addr(helper)[:2]
            n = engines(core, helper)
            g.remote_dma(T.relay[:], T.out[:], T.sem.got, T.sem.arrived, pid, rid, (1 << n) - 1)
        expected += n
    for route in take:
        expected += engines(route[1], core)
    if expected:
        g.wait_ge(T.sem.arrived, expected)
    if take:
        g.dma_start(T.y[:], T.land[:]).then_inc(T.sem.stored, 16)
        g.wait_ge(T.sem.stored, 16)
